import numpy as np
import ml_dtypes


def mxq(x, axis, fmt="e4m3"):
    dtype, down = {"e4m3": (ml_dtypes.float8_e4m3fn, 7), "e5m2": (ml_dtypes.float8_e5m2, 14)}[fmt]
    v = np.moveaxis(np.asarray(x, np.float32).astype(ml_dtypes.bfloat16).astype(np.float64), axis, -1)
    blocks = v.reshape(v.shape[:-1] + (-1, 32))
    amax = np.abs(blocks).max(-1, keepdims=True)
    byte = np.maximum(np.where(amax > 0, np.frexp(amax)[1] - 1 + 127, 0) - down, 1)
    scale = np.exp2(byte - 127.0)
    codes = (blocks / scale).astype(np.float32).astype(dtype).astype(np.float64)
    return np.moveaxis((codes * scale).reshape(v.shape), -1, axis)


WIDE = False


def mx_kscale(k):
    if not WIDE:
        return np.ones(k)
    levels = np.array([10, -10, 5, -5, 0])
    if k % 512:
        return np.exp2(np.random.permutation(np.resize(levels, k // 32))).repeat(32)
    a = np.empty((k // 512, 16))
    for p in range(k // 512):
        a[p, :8] = np.random.permutation(np.resize(levels, 8))
        for g in range(8):
            far = levels[np.abs(levels - a[p, g]) >= 10]
            a[p, g + 8] = far[np.random.randint(len(far))]
    return np.exp2(a.ravel()).repeat(32)


def f64(x):
    return np.asarray(x).astype(np.float64)


def striped(idx):
    return np.tile(idx.reshape(-1, 16).T, (8, 1)).astype(np.uint16)


def unstriped(offs):
    return offs[:16].T.reshape(-1).astype(np.int64)


def pack_weight(w):
    k, n = w.shape
    w = f64(np.asarray(w, np.float32).astype(ml_dtypes.bfloat16)).reshape(k // 32, 32, n)
    amax = np.abs(w).max(1)
    byte = np.clip(np.where(amax > 0, np.frexp(amax)[1] - 1 + 127 - 7, 1), 1, 254)
    scaled = (w * np.exp2(127.0 - byte)[:, None, :]).reshape(k, n).astype(np.float32)
    words = np.ascontiguousarray(scaled.reshape(k // 512, 128, 4, n).transpose(0, 1, 3, 2)).astype(ml_dtypes.float8_e4m3fn).view(np.uint8)
    return words, np.ascontiguousarray(byte.astype(np.uint8).reshape(k // 512, 16, n))


def unpack_weight(words, scales):
    g, p, n, _ = words.shape
    vals = np.ascontiguousarray(words).view(ml_dtypes.float8_e4m3fn).astype(np.float64) * np.repeat(np.exp2(scales.astype(np.float64) - 127.0), 8, axis=1)[..., None]
    return vals.transpose(0, 1, 3, 2).reshape(g * 512, n)


def relu(v):
    return np.maximum(v, 0.0)


def sigmoid(v):
    return 1.0 / (1.0 + np.exp(-np.maximum(v, -700.0)))


K, T, S, H, N, W = 512, 1024, 512, 512, 128, 2048
P = 2 ** 7


def setup_inputs():
    n = np.random.standard_normal
    s = mx_kscale(K)[:, None]
    u = mx_kscale(H)
    packed_xT = pack_weight(n((K, T)) * s)
    packed_eT = pack_weight(n((K, W)) * s)
    return {
        "x_words": packed_xT[0],
        "x_scales": packed_xT[1],
        "e_words": packed_eT[0],
        "e_scales": packed_eT[1],
        "w1": (n((K, H)) / np.sqrt(2 * K) / s * u).astype(np.float32),
        "w2": (n((K, H)) / np.sqrt(2 * K) / s * u).astype(np.float32),
        "w3": (n((H, N)) / np.sqrt(H) / u[:, None]).astype(np.float32),
        "al": (np.tile(np.random.uniform(0.0, 1.0, S), (P, 1))).astype(np.float32),
        "be": (np.tile(np.random.uniform(0.0, 1.0, S), (P, 1))).astype(np.float32),
        "offs": striped(np.random.permutation(T)[:S]),
        "far": striped(np.random.permutation(T)[:S]),
        "fine": striped(np.random.permutation(W)[:S]),
        "ffar": striped(np.random.permutation(W)[:S]),
    }


def reference(x_words, x_scales, e_words, e_scales, w1, w2, w3, al, be, offs, far, fine, ffar):
    xq = unpack_weight(x_words, x_scales)[:, unstriped(offs)]
    w1q = mxq(f64(w1), 0, "e4m3")
    y = w1q.T @ xq
    x_far = unpack_weight(x_words, x_scales)[:, unstriped(far)]
    yf = w1q.T @ x_far
    e_fine = unpack_weight(e_words, e_scales)[:, unstriped(fine)]
    w2q = mxq(f64(w2), 0, "e4m3")
    p = w2q.T @ e_fine
    e_ffar = unpack_weight(e_words, e_scales)[:, unstriped(ffar)]
    pf = w2q.T @ e_ffar
    h = relu(y + f64(al)[:1] * (yf - y) + p + f64(be)[:1] * (pf - p))
    return sigmoid(mxq(f64(w3), 0, "e4m3").T @ mxq(h, 0, "e4m3"))

@@ -1,0 +1,200 @@
+from contextlib import ExitStack
+
+import concourse.mybir as mybir
+from concourse.masks import make_identity
+
+K, T, S, H, N, W = 512, 1024, 512, 512, 128, 2048
+FLOPS = 2 * (4 * K * H * S + H * N * S)
+
+F32 = mybir.dt.float32
+BF16 = mybir.dt.bfloat16
+I32 = mybir.dt.int32
+U32 = mybir.dt.uint32
+U16 = mybir.dt.uint16
+U8 = mybir.dt.uint8
+FP8X4 = mybir.dt.float8_e4m3fn_x4
+ACT = mybir.ActivationFunctionType
+ALU = mybir.AluOpType
+
+P = 128
+PACK = 4
+TILES = S // P
+HALF = H // 2
+
+
+def tile_picked_yngp_sigmoid_p_kernel(tc, x_words, x_scales, e_words, e_scales, w1, w2, w3, al, be, offs, far, fine, ffar, out):
+    nc = tc.nc
+    with ExitStack() as ctx:
+        keep = ctx.enter_context(tc.tile_pool(name="keep", bufs=1))
+        products = ctx.enter_context(tc.psum_pool(name="products", bufs=4))
+        sums = ctx.enter_context(tc.psum_pool(name="sums", bufs=1))
+
+        def load_list(name, src):
+            tile = keep.tile([P, S // 16], U16, name=name)
+            nc.sync.dma_start(tile[:], src)
+            return tile
+
+        def load_scales(name, src, width, queue):
+            tile = keep.tile([P, width], U8, name=name, align_bytes=64)
+            nc.gpsimd.memset(tile[:].bitcast(I32), 0)
+            for q in range(4):
+                queue.dma_start(tile[32 * q : 32 * q + 4, :].bitcast(I32), src[0, 4 * q : 4 * q + 4, :].bitcast(I32))
+            return tile
+
+        def load_words(name, src, width):
+            tile = keep.tile([P, width], U32, name=name, align_bytes=64)
+            nc.sync.dma_start(tile[:].bitcast(I32), src[0].rearrange("p n t -> p (n t)").bitcast(I32))
+            return tile
+
+        def load_weight(name, src):
+            width = src.shape[1]
+            tile = keep.tile([P, PACK, width], F32, name=name)
+            nc.sync.dma_start(tile[:], src.rearrange("(p t) c -> p t c", t=PACK))
+            return tile
+
+        def gather(name, table, offsets, dtype, tag=None):
+            tile = keep.tile([P, 16 * offsets.shape[1]], dtype, name=name, tag=tag or name, align_bytes=64)
+            nc.vector.tensor_copy(tile[:], table[:].indirect(offsets))
+            return tile
+
+        def interleave(name, raw):
+            width = raw.shape[2]
+            tile = keep.tile([P, width * PACK], BF16, name=name, align_bytes=64)
+            nc.scalar.copy(
+                tile[:].rearrange("p (c i t) -> p c t i", i=4, t=PACK),
+                raw[:].rearrange("p t (c i) -> p c t i", i=4),
+            )
+            return tile
+
+        def quantize(name, parts):
+            width = sum(part.shape[1] for part in parts) // PACK
+            codes = keep.tile([P, width], U32, name=name + "_codes", align_bytes=64)
+            scales = keep.tile([P, width], U8, name=name + "_scales", align_bytes=64)
+            at = 0
+            for part in parts:
+                cols = slice(at, at + part.shape[1] // PACK)
+                nc.vector.quantize_mx(out=codes[:, cols].bitcast(FP8X4), scales=scales[:, cols], in_=part[:])
+                at = cols.stop
+            return codes, scales
+
+        xs = load_scales("xs", x_scales, T, nc.scalar)
+        offs_t = load_list("offs_t", offs)
+        xw = load_words("xw", x_words, T)
+        far_t = load_list("far_t", far)
+        w1_raw = [load_weight("w1_raw%d" % h, w1[:, h * HALF : (h + 1) * HALF]) for h in range(2)]
+        w2_raw = [load_weight("w2_raw%d" % h, w2[:, h * HALF : (h + 1) * HALF]) for h in range(2)]
+        fine_t = load_list("fine_t", fine)
+        ffar_t = load_list("ffar_t", ffar)
+        es = load_scales("es", e_scales, W, nc.sync)
+        ew = load_words("ew", e_words, W)
+        w3_raw = load_weight("w3_raw", w3)
+
+        warm = keep.tile([P, 1], F32, name="warm")
+        nc.gpsimd.memset(warm[:], 0.0)
+        warm_out = keep.tile([P, 1], F32, name="warm_out")
+        nc.scalar.activation(warm_out[:], warm[:], ACT.Sigmoid)
+
+        rows = keep.tile([P, P], F32, name="rows")
+        nc.gpsimd.memset(rows[:], 0.0)
+        nc.gpsimd.dma_start(rows[0:TILES, :], al[0].rearrange("(r c) -> r c", r=TILES))
+        nc.gpsimd.dma_start(rows[TILES : 2 * TILES, :], be[0].rearrange("(r c) -> r c", r=TILES))
+        ident = keep.tile([P, P], F32, name="ident")
+        make_identity(nc, ident[:])
+        turned = products.tile([P, S], F32, name="product")
+        nc.tensor.transpose(turned[:, 0:P], rows[:], ident[:])
+        far_w = keep.tile([P, 2 * TILES], F32, name="far_w")
+        near_w = keep.tile([P, 2 * TILES], F32, name="near_w")
+        nc.scalar.copy(far_w[:], turned[:, 0 : 2 * TILES])
+        nc.scalar.activation(near_w[:], turned[:, 0 : 2 * TILES], ACT.Copy, bias=1.0, scale=-1.0)
+
+        near_x = (gather("near_xw", xw, offs_t[:], U32), gather("near_xs", xs, offs_t[:], U8))
+        w1_bf = [interleave("w1_bf%d" % h, w1_raw[h]) for h in range(2)]
+        w1_q = quantize("w1", w1_bf)
+        far_x = (gather("far_xw", xw, far_t[:], U32, tag="w1_bf1"), gather("far_xs", xs, far_t[:], U8, tag="w1_bf0"))
+        w2_bf = [interleave("w2_bf%d" % h, w2_raw[h]) for h in range(2)]
+        near_es = gather("near_es", es, fine_t[:], U8)
+        far_es = gather("far_es", es, ffar_t[:], U8)
+        w2_q = quantize("w2", w2_bf)
+        near_e = (gather("near_ew", ew, fine_t[:], U32, tag="w2_bf1"), near_es)
+        far_ew = [gather("far_ew%d" % h, ew, ffar_t[:, 16 * h : 16 * (h + 1)], U32) for h in range(2)]
+
+        def project(words, scales, weight):
+            product = products.tile([P, H], F32, name="product")
+            nc.tensor.matmul_mx(
+                out=product[:],
+                lhsT=words.bitcast(FP8X4),
+                lhsT_scale=scales,
+                rhs=weight[0][:].bitcast(FP8X4),
+                rhs_scale=weight[1][:],
+                start=True,
+                stop=True,
+            )
+            return product[:].rearrange("p (m t) -> p t m", t=PACK)
+
+        def samples(jt):
+            return slice(jt * P, (jt + 1) * P)
+
+        def scaled(name, product, factor):
+            term = keep.tile([P, PACK, P], F32, name=name)
+            nc.scalar.activation(term[:], product, ACT.Copy, scale=factor)
+            return term
+
+        def scaled_onto(name, product, factor, other):
+            term = keep.tile([P, PACK, P], F32, name=name)
+            nc.vector.scalar_tensor_tensor(term[:], product, factor, other[:], ALU.mult, ALU.add)
+            return term
+
+        totals = [sums.tile([P, PACK, P], F32, name="total%d" % jt) for jt in range(TILES)]
+
+        def turn(term, jt, first, last):
+            for t in range(PACK):
+                nc.tensor.matmul(
+                    totals[jt][:, t, :], term[:, t, :], ident[:],
+                    start=(first and t == 0), stop=(last and t == PACK - 1), is_transpose=True,
+                )
+
+        near_y = []
+        for jt in range(TILES):
+            product = project(near_x[0][:, samples(jt)], near_x[1][:, samples(jt)], w1_q)
+            near_y.append(scaled("near_y%d" % jt, product, near_w[:, jt : jt + 1]))
+        far_y = []
+        for jt in range(TILES):
+            product = project(far_x[0][:, samples(jt)], far_x[1][:, samples(jt)], w1_q)
+            far_y.append(scaled("far_y%d" % jt, product, far_w[:, jt : jt + 1]))
+        w3_bf = interleave("w3_bf", w3_raw)
+        near_p = []
+        for jt in range(TILES):
+            product = project(near_e[0][:, samples(jt)], near_e[1][:, samples(jt)], w2_q)
+            near_p.append(scaled("near_p%d" % jt, product, near_w[:, TILES + jt : TILES + jt + 1]))
+        for jt in range(TILES):
+            turn(near_y[jt], jt, True, False)
+        for jt in range(TILES):
+            turn(far_y[jt], jt, False, False)
+        last = []
+        for jt in range(TILES):
+            product = project(far_ew[jt // 2][:, samples(jt % 2)], far_es[:, samples(jt)], w2_q)
+            last.append(scaled_onto("far_p%d" % jt, product, far_w[:, TILES + jt : TILES + jt + 1], near_p[jt]))
+        w3_q = quantize("w3", [w3_bf])
+        hidden = []
+        for jt in range(TILES):
+            turn(last[jt], jt, False, True)
+            tile = keep.tile([P, P * PACK], BF16, name="hidden%d" % jt, align_bytes=64)
+            nc.scalar.activation(
+                tile[:].rearrange("p (j t) -> p j t", t=PACK), totals[jt][:].rearrange("p t j -> p j t"), ACT.Relu
+            )
+            hidden.append(tile)
+        for jt in range(TILES):
+            h_q = quantize("h%d" % jt, [hidden[jt]])
+            logits = products.tile([P, H], F32, name="product")
+            nc.tensor.matmul_mx(
+                out=logits[:, 0:P],
+                lhsT=w3_q[0][:].bitcast(FP8X4),
+                lhsT_scale=w3_q[1][:],
+                rhs=h_q[0][:].bitcast(FP8X4),
+                rhs_scale=h_q[1][:],
+                start=True,
+                stop=True,
+            )
+            result = keep.tile([P, P], F32, name="result%d" % jt)
+            nc.scalar.activation(result[:], logits[:, 0:P], ACT.Sigmoid)
+            nc.sync.dma_start(out[:, samples(jt)], result[:])

@@ -20,24 +20,25 @@ P = 128
 PACK = 4
 TILES = S // P
 HALF = H // 2
+SCALAR_RELUS = 4
+GROUPS = ((0, 1), (2,), (3,))
 
 
 def tile_picked_yngp_sigmoid_p_kernel(tc, x_words, x_scales, e_words, e_scales, w1, w2, w3, al, be, offs, far, fine, ffar, out):
     nc = tc.nc
     with ExitStack() as ctx:
         keep = ctx.enter_context(tc.tile_pool(name="keep", bufs=1))
-        products = ctx.enter_context(tc.psum_pool(name="products", bufs=4))
-        sums = ctx.enter_context(tc.psum_pool(name="sums", bufs=1))
+        products = ctx.enter_context(tc.psum_pool(name="products", bufs=1))
 
         def load_list(name, src):
             tile = keep.tile([P, S // 16], U16, name=name)
             nc.sync.dma_start(tile[:], src)
             return tile
 
-        def load_scales(name, src, width, queue):
+        def load_scales(name, src, width, queues):
             tile = keep.tile([P, width], U8, name=name, align_bytes=64)
-            nc.gpsimd.memset(tile[:].bitcast(I32), 0)
-            for q in range(4):
+            nc.vector.memset(tile[:].bitcast(I32), 0)
+            for q, queue in enumerate(queues):
                 queue.dma_start(tile[32 * q : 32 * q + 4, :].bitcast(I32), src[0, 4 * q : 4 * q + 4, :].bitcast(I32))
             return tile
 
@@ -48,7 +49,7 @@ def tile_picked_yngp_sigmoid_p_kernel(tc, x_words, x_scales, e_words, e_scales, 
 
         def load_weight(name, src):
             width = src.shape[1]
-            tile = keep.tile([P, PACK, width], F32, name=name)
+            tile = keep.tile([P, PACK, width], F32, name=name, align_bytes=64)
             nc.sync.dma_start(tile[:], src.rearrange("(p t) c -> p t c", t=PACK))
             return tile
 
@@ -57,10 +58,10 @@ def tile_picked_yngp_sigmoid_p_kernel(tc, x_words, x_scales, e_words, e_scales, 
             nc.vector.tensor_copy(tile[:], table[:].indirect(offsets))
             return tile
 
-        def interleave(name, raw):
+        def interleave(name, raw, copy, tag=None):
             width = raw.shape[2]
-            tile = keep.tile([P, width * PACK], BF16, name=name, align_bytes=64)
-            nc.scalar.copy(
+            tile = keep.tile([P, width * PACK], BF16, name=name, tag=tag or name, align_bytes=64)
+            copy(
                 tile[:].rearrange("p (c i t) -> p c t i", i=4, t=PACK),
                 raw[:].rearrange("p t (c i) -> p c t i", i=4),
             )
@@ -77,49 +78,48 @@ def tile_picked_yngp_sigmoid_p_kernel(tc, x_words, x_scales, e_words, e_scales, 
                 at = cols.stop
             return codes, scales
 
-        xs = load_scales("xs", x_scales, T, nc.scalar)
+        rows = keep.tile([P, P], F32, name="rows", tag="w1_codes", align_bytes=64)
+        nc.gpsimd.memset(rows[:], 0.0)
+        nc.gpsimd.dma_start(rows[0:TILES, :], al[0].rearrange("(r c) -> r c", r=TILES))
+        nc.gpsimd.dma_start(rows[TILES : 2 * TILES, :], be[0].rearrange("(r c) -> r c", r=TILES))
+        xs = load_scales("xs", x_scales, T, (nc.sync, nc.sync, nc.scalar, nc.scalar))
         offs_t = load_list("offs_t", offs)
-        xw = load_words("xw", x_words, T)
         far_t = load_list("far_t", far)
-        w1_raw = [load_weight("w1_raw%d" % h, w1[:, h * HALF : (h + 1) * HALF]) for h in range(2)]
-        w2_raw = [load_weight("w2_raw%d" % h, w2[:, h * HALF : (h + 1) * HALF]) for h in range(2)]
+        w1_raw = [load_weight("w1_raw0", w1[:, :HALF])]
+        xw = load_words("xw", x_words, T)
+        w1_raw.append(load_weight("w1_raw1", w1[:, HALF:]))
         fine_t = load_list("fine_t", fine)
+        es = load_scales("es", e_scales, W, (nc.sync,) * 4)
+        w2_raw = [load_weight("w2_raw%d" % h, w2[:, h * HALF : (h + 1) * HALF]) for h in range(2)]
         ffar_t = load_list("ffar_t", ffar)
-        es = load_scales("es", e_scales, W, nc.sync)
         ew = load_words("ew", e_words, W)
         w3_raw = load_weight("w3_raw", w3)
 
         warm = keep.tile([P, 1], F32, name="warm")
-        nc.gpsimd.memset(warm[:], 0.0)
+        nc.vector.memset(warm[:], 0.0)
         warm_out = keep.tile([P, 1], F32, name="warm_out")
         nc.scalar.activation(warm_out[:], warm[:], ACT.Sigmoid)
 
-        rows = keep.tile([P, P], F32, name="rows")
-        nc.gpsimd.memset(rows[:], 0.0)
-        nc.gpsimd.dma_start(rows[0:TILES, :], al[0].rearrange("(r c) -> r c", r=TILES))
-        nc.gpsimd.dma_start(rows[TILES : 2 * TILES, :], be[0].rearrange("(r c) -> r c", r=TILES))
         ident = keep.tile([P, P], F32, name="ident")
         make_identity(nc, ident[:])
-        turned = products.tile([P, S], F32, name="product")
+        turned = products.tile([P, S], F32, name="turned", tag="bank7")
         nc.tensor.transpose(turned[:, 0:P], rows[:], ident[:])
-        far_w = keep.tile([P, 2 * TILES], F32, name="far_w")
-        near_w = keep.tile([P, 2 * TILES], F32, name="near_w")
-        nc.scalar.copy(far_w[:], turned[:, 0 : 2 * TILES])
-        nc.scalar.activation(near_w[:], turned[:, 0 : 2 * TILES], ACT.Copy, bias=1.0, scale=-1.0)
 
-        near_x = (gather("near_xw", xw, offs_t[:], U32), gather("near_xs", xs, offs_t[:], U8))
-        w1_bf = [interleave("w1_bf%d" % h, w1_raw[h]) for h in range(2)]
+        near_xs = gather("near_xs", xs, offs_t[:], U8)
+        far_xs = gather("far_xs", xs, far_t[:], U8)
+        near_x = (gather("near_xw", xw, offs_t[:], U32), near_xs)
+        far_x = (gather("far_xw", xw, far_t[:], U32), far_xs)
+        w1_bf = [interleave("w1_bf%d" % h, w1_raw[h], nc.scalar.copy) for h in range(2)]
         w1_q = quantize("w1", w1_bf)
-        far_x = (gather("far_xw", xw, far_t[:], U32, tag="w1_bf1"), gather("far_xs", xs, far_t[:], U8, tag="w1_bf0"))
-        w2_bf = [interleave("w2_bf%d" % h, w2_raw[h]) for h in range(2)]
-        near_es = gather("near_es", es, fine_t[:], U8)
-        far_es = gather("far_es", es, ffar_t[:], U8)
-        w2_q = quantize("w2", w2_bf)
-        near_e = (gather("near_ew", ew, fine_t[:], U32, tag="w2_bf1"), near_es)
-        far_ew = [gather("far_ew%d" % h, ew, ffar_t[:, 16 * h : 16 * (h + 1)], U32) for h in range(2)]
+        w2_bf = [interleave("w2_bf%d" % h, w2_raw[h], nc.scalar.copy) for h in range(2)]
+        factors = keep.tile([P, 2, 2 * TILES], F32, name="factors", tag="w1_bf1", align_bytes=64)
+        far_w = factors[:, 0, :]
+        near_w = factors[:, 1, :]
+        nc.vector.tensor_copy(far_w, turned[:, 0 : 2 * TILES])
+        nc.vector.tensor_scalar(near_w, turned[:, 0 : 2 * TILES], -1.0, 1.0, ALU.mult, ALU.add)
 
-        def project(words, scales, weight):
-            product = products.tile([P, H], F32, name="product")
+        def project(words, scales, weight, bank):
+            product = products.tile([P, H], F32, name="product", tag="bank%d" % bank)
             nc.tensor.matmul_mx(
                 out=product[:],
                 lhsT=words.bitcast(FP8X4),
@@ -134,67 +134,115 @@ def tile_picked_yngp_sigmoid_p_kernel(tc, x_words, x_scales, e_words, e_scales, 
         def samples(jt):
             return slice(jt * P, (jt + 1) * P)
 
-        def scaled(name, product, factor):
-            term = keep.tile([P, PACK, P], F32, name=name)
-            nc.scalar.activation(term[:], product, ACT.Copy, scale=factor)
+        def term_tile(name, tag=None):
+            return keep.tile([P, PACK, P], F32, name=name, tag=tag or name, align_bytes=64)
+
+        def scaled(term, product, factor):
+            nc.scalar.activation(term, product, ACT.Copy, scale=factor)
             return term
 
-        def scaled_onto(name, product, factor, other):
-            term = keep.tile([P, PACK, P], F32, name=name)
-            nc.vector.scalar_tensor_tensor(term[:], product, factor, other[:], ALU.mult, ALU.add)
+        def scaled_onto(term, product, factor, other):
+            nc.vector.scalar_tensor_tensor(term, product, factor, other, ALU.mult, ALU.add)
             return term
 
-        totals = [sums.tile([P, PACK, P], F32, name="total%d" % jt) for jt in range(TILES)]
+        totals = {}
 
         def turn(term, jt, first, last):
+            if first:
+                totals[jt] = products.tile([P, PACK, P], F32, name="total%d" % jt, tag="bank%d" % jt)
             for t in range(PACK):
                 nc.tensor.matmul(
                     totals[jt][:, t, :], term[:, t, :], ident[:],
                     start=(first and t == 0), stop=(last and t == PACK - 1), is_transpose=True,
                 )
 
-        near_y = []
-        for jt in range(TILES):
-            product = project(near_x[0][:, samples(jt)], near_x[1][:, samples(jt)], w1_q)
-            near_y.append(scaled("near_y%d" % jt, product, near_w[:, jt : jt + 1]))
-        far_y = []
-        for jt in range(TILES):
-            product = project(far_x[0][:, samples(jt)], far_x[1][:, samples(jt)], w1_q)
-            far_y.append(scaled("far_y%d" % jt, product, far_w[:, jt : jt + 1]))
-        w3_bf = interleave("w3_bf", w3_raw)
-        near_p = []
-        for jt in range(TILES):
-            product = project(near_e[0][:, samples(jt)], near_e[1][:, samples(jt)], w2_q)
-            near_p.append(scaled("near_p%d" % jt, product, near_w[:, TILES + jt : TILES + jt + 1]))
-        for jt in range(TILES):
-            turn(near_y[jt], jt, True, False)
-        for jt in range(TILES):
-            turn(far_y[jt], jt, False, False)
-        last = []
-        for jt in range(TILES):
-            product = project(far_ew[jt // 2][:, samples(jt % 2)], far_es[:, samples(jt)], w2_q)
-            last.append(scaled_onto("far_p%d" % jt, product, far_w[:, TILES + jt : TILES + jt + 1], near_p[jt]))
-        w3_q = quantize("w3", [w3_bf])
-        hidden = []
-        for jt in range(TILES):
+        near_es = gather("near_es", es, fine_t[:], U8, tag="w1_bf0")
+        far_es = gather("far_es", es, ffar_t[:], U8)
+        w2_q = quantize("w2", w2_bf)
+        near_ew = gather("near_ew", ew, fine_t[:], U32, tag="w2_bf1")
+        far_ew = [gather("far_ew%d" % h, ew, ffar_t[:, 16 * h : 16 * (h + 1)], U32) for h in range(2)]
+
+        coarse = keep.tile([P, 2 * TILES, PACK, P], F32, name="coarse", tag="w2_raw1", align_bytes=64)
+        near_y = coarse[:, :TILES]
+        far_y, near_p, last = {}, {}, {}
+
+        def near_coarse(jt):
+            product = project(near_x[0][:, samples(jt)], near_x[1][:, samples(jt)], w1_q, jt)
+            scaled(near_y[:, jt], product, near_w[:, jt : jt + 1])
+
+        def far_coarse(jt):
+            product = project(far_x[0][:, samples(jt)], far_x[1][:, samples(jt)], w1_q, TILES + jt)
+            far_y[jt] = scaled(coarse[:, TILES + jt], product, far_w[:, jt : jt + 1])
+
+        def near_fine(jt, bank, chained, tag=None):
+            product = project(near_ew[:, samples(jt)], near_es[:, samples(jt)], w2_q, TILES + bank)
+            factor = near_w[:, TILES + jt : TILES + jt + 1]
+            if chained:
+                near_p[jt] = scaled_onto(term_tile("near_p%d" % jt, tag)[:], product, factor, far_y[jt])
+            else:
+                near_p[jt] = scaled(term_tile("near_p%d" % jt)[:], product, factor)
+
+        def far_fine(jt, bank, chained=True):
+            product = project(far_ew[jt // 2][:, samples(jt % 2)], far_es[:, samples(jt)], w2_q, TILES + bank)
+            factor = far_w[:, TILES + jt : TILES + jt + 1]
+            if chained:
+                last[jt] = scaled_onto(term_tile("far_p%d" % jt)[:], product, factor, near_p[jt])
+            else:
+                last[jt] = scaled(term_tile("far_p%d" % jt)[:], product, factor)
+
+        hidden = [keep.tile([P, len(group), P, PACK], BF16, name="hidden%d" % group[0], align_bytes=64) for group in GROUPS]
+
+        def rectify(jt):
             turn(last[jt], jt, False, True)
-            tile = keep.tile([P, P * PACK], BF16, name="hidden%d" % jt, align_bytes=64)
-            nc.scalar.activation(
-                tile[:].rearrange("p (j t) -> p j t", t=PACK), totals[jt][:].rearrange("p t j -> p j t"), ACT.Relu
-            )
-            hidden.append(tile)
-        for jt in range(TILES):
-            h_q = quantize("h%d" % jt, [hidden[jt]])
-            logits = products.tile([P, H], F32, name="product")
+            total = totals[jt][:].rearrange("p t j -> p j t")
+            target = [tile[:, group.index(jt)] for group, tile in zip(GROUPS, hidden) if jt in group][0]
+            if jt < SCALAR_RELUS:
+                nc.scalar.activation(target, total, ACT.Relu)
+            else:
+                nc.vector.tensor_scalar_max(target, total, 0.0)
+
+        near_coarse(0)
+        near_coarse(1)
+        near_coarse(2)
+        near_coarse(3)
+        far_coarse(0)
+        far_coarse(1)
+        far_coarse(2)
+        far_coarse(3)
+        turn(near_y[:, 0], 0, True, False)
+        turn(near_y[:, 1], 1, True, False)
+        turn(near_y[:, 2], 2, True, False)
+        turn(near_y[:, 3], 3, True, False)
+        turn(far_y[0], 0, False, False)
+        near_fine(0, 0, False)
+        near_fine(2, 1, True, "ew")
+        turn(far_y[1], 1, False, False)
+        near_fine(3, 2, True)
+        near_fine(1, 3, False)
+        far_fine(0, 1)
+        far_fine(1, 0)
+        far_fine(2, 2)
+        rectify(0)
+        far_fine(3, 3)
+        w3_q = quantize("w3", [interleave("w3_bf", w3_raw, nc.scalar.copy, tag="near_p0")])
+        rectify(1)
+        rectify(2)
+        rectify(3)
+        for group, tile in zip(GROUPS, hidden):
+            width = len(group) * P
+            codes = keep.tile([P, width], U32, name="h_codes%d" % group[0], align_bytes=64)
+            scales = keep.tile([P, width], U8, name="h_scales%d" % group[0], align_bytes=64)
+            nc.vector.quantize_mx(out=codes[:].bitcast(FP8X4), scales=scales[:], in_=tile[:].rearrange("p g j t -> p (g j t)"))
+            logits = products.tile([P, H], F32, name="logits", tag="bank%d" % (TILES + group[0]))
             nc.tensor.matmul_mx(
-                out=logits[:, 0:P],
+                out=logits[:, 0:width],
                 lhsT=w3_q[0][:].bitcast(FP8X4),
                 lhsT_scale=w3_q[1][:],
-                rhs=h_q[0][:].bitcast(FP8X4),
-                rhs_scale=h_q[1][:],
+                rhs=codes[:].bitcast(FP8X4),
+                rhs_scale=scales[:],
                 start=True,
                 stop=True,
             )
-            result = keep.tile([P, P], F32, name="result%d" % jt)
-            nc.scalar.activation(result[:], logits[:, 0:P], ACT.Sigmoid)
-            nc.sync.dma_start(out[:, samples(jt)], result[:])
+            result = keep.tile([P, width], F32, name="result%d" % group[0])
+            nc.scalar.activation(result[:], logits[:, 0:width], ACT.Sigmoid)
+            nc.sync.dma_start(out[:, group[0] * P : group[0] * P + width], result[:])

from contextlib import ExitStack

import concourse.mybir as mybir
from concourse.masks import make_identity

K, T, S, H, N, W = 512, 1024, 512, 512, 128, 2048
FLOPS = 2 * (4 * K * H * S + H * N * S)

F32 = mybir.dt.float32
BF16 = mybir.dt.bfloat16
I32 = mybir.dt.int32
U32 = mybir.dt.uint32
U16 = mybir.dt.uint16
U8 = mybir.dt.uint8
FP8X4 = mybir.dt.float8_e4m3fn_x4
ACT = mybir.ActivationFunctionType
ALU = mybir.AluOpType

P = 128
PACK = 4
TILES = S // P
HALF = H // 2
SCALAR_RELUS = 4
GROUPS = ((0, 1), (2,), (3,))


def tile_picked_yngp_sigmoid_p_kernel(tc, x_words, x_scales, e_words, e_scales, w1, w2, w3, al, be, offs, far, fine, ffar, out):
    nc = tc.nc
    with ExitStack() as ctx:
        keep = ctx.enter_context(tc.tile_pool(name="keep", bufs=1))
        products = ctx.enter_context(tc.psum_pool(name="products", bufs=1))

        def load_list(name, src):
            tile = keep.tile([P, S // 16], U16, name=name)
            nc.sync.dma_start(tile[:], src)
            return tile

        def load_scales(name, src, width, queues):
            tile = keep.tile([P, width], U8, name=name, align_bytes=64)
            nc.vector.memset(tile[:].bitcast(I32), 0)
            for q, queue in enumerate(queues):
                queue.dma_start(tile[32 * q : 32 * q + 4, :].bitcast(I32), src[0, 4 * q : 4 * q + 4, :].bitcast(I32))
            return tile

        def load_words(name, src, width):
            tile = keep.tile([P, width], U32, name=name, align_bytes=64)
            nc.sync.dma_start(tile[:].bitcast(I32), src[0].rearrange("p n t -> p (n t)").bitcast(I32))
            return tile

        def load_weight(name, src):
            width = src.shape[1]
            tile = keep.tile([P, PACK, width], F32, name=name, align_bytes=64)
            nc.sync.dma_start(tile[:], src.rearrange("(p t) c -> p t c", t=PACK))
            return tile

        def gather(name, table, offsets, dtype, tag=None):
            tile = keep.tile([P, 16 * offsets.shape[1]], dtype, name=name, tag=tag or name, align_bytes=64)
            nc.vector.tensor_copy(tile[:], table[:].indirect(offsets))
            return tile

        def interleave(name, raw, copy, tag=None):
            width = raw.shape[2]
            tile = keep.tile([P, width * PACK], BF16, name=name, tag=tag or name, align_bytes=64)
            copy(
                tile[:].rearrange("p (c i t) -> p c t i", i=4, t=PACK),
                raw[:].rearrange("p t (c i) -> p c t i", i=4),
            )
            return tile

        def quantize(name, parts):
            width = sum(part.shape[1] for part in parts) // PACK
            codes = keep.tile([P, width], U32, name=name + "_codes", align_bytes=64)
            scales = keep.tile([P, width], U8, name=name + "_scales", align_bytes=64)
            at = 0
            for part in parts:
                cols = slice(at, at + part.shape[1] // PACK)
                nc.vector.quantize_mx(out=codes[:, cols].bitcast(FP8X4), scales=scales[:, cols], in_=part[:])
                at = cols.stop
            return codes, scales

        rows = keep.tile([P, P], F32, name="rows", tag="w1_codes", align_bytes=64)
        nc.gpsimd.memset(rows[:], 0.0)
        nc.gpsimd.dma_start(rows[0:TILES, :], al[0].rearrange("(r c) -> r c", r=TILES))
        nc.gpsimd.dma_start(rows[TILES : 2 * TILES, :], be[0].rearrange("(r c) -> r c", r=TILES))
        xs = load_scales("xs", x_scales, T, (nc.sync, nc.sync, nc.scalar, nc.scalar))
        offs_t = load_list("offs_t", offs)
        far_t = load_list("far_t", far)
        w1_raw = [load_weight("w1_raw0", w1[:, :HALF])]
        xw = load_words("xw", x_words, T)
        w1_raw.append(load_weight("w1_raw1", w1[:, HALF:]))
        fine_t = load_list("fine_t", fine)
        es = load_scales("es", e_scales, W, (nc.sync,) * 4)
        w2_raw = [load_weight("w2_raw%d" % h, w2[:, h * HALF : (h + 1) * HALF]) for h in range(2)]
        ffar_t = load_list("ffar_t", ffar)
        ew = load_words("ew", e_words, W)
        w3_raw = load_weight("w3_raw", w3)

        warm = keep.tile([P, 1], F32, name="warm")
        nc.vector.memset(warm[:], 0.0)
        warm_out = keep.tile([P, 1], F32, name="warm_out")
        nc.scalar.activation(warm_out[:], warm[:], ACT.Sigmoid)

        ident = keep.tile([P, P], F32, name="ident")
        make_identity(nc, ident[:])
        turned = products.tile([P, S], F32, name="turned", tag="bank7")
        nc.tensor.transpose(turned[:, 0:P], rows[:], ident[:])

        near_xs = gather("near_xs", xs, offs_t[:], U8)
        far_xs = gather("far_xs", xs, far_t[:], U8)
        near_x = (gather("near_xw", xw, offs_t[:], U32), near_xs)
        far_x = (gather("far_xw", xw, far_t[:], U32), far_xs)
        w1_bf = [interleave("w1_bf%d" % h, w1_raw[h], nc.scalar.copy) for h in range(2)]
        w1_q = quantize("w1", w1_bf)
        w2_bf = [interleave("w2_bf%d" % h, w2_raw[h], nc.scalar.copy) for h in range(2)]
        factors = keep.tile([P, 2, 2 * TILES], F32, name="factors", tag="w1_bf1", align_bytes=64)
        far_w = factors[:, 0, :]
        near_w = factors[:, 1, :]
        nc.vector.tensor_copy(far_w, turned[:, 0 : 2 * TILES])
        nc.vector.tensor_scalar(near_w, turned[:, 0 : 2 * TILES], -1.0, 1.0, ALU.mult, ALU.add)

        def project(words, scales, weight, bank):
            product = products.tile([P, H], F32, name="product", tag="bank%d" % bank)
            nc.tensor.matmul_mx(
                out=product[:],
                lhsT=words.bitcast(FP8X4),
                lhsT_scale=scales,
                rhs=weight[0][:].bitcast(FP8X4),
                rhs_scale=weight[1][:],
                start=True,
                stop=True,
            )
            return product[:].rearrange("p (m t) -> p t m", t=PACK)

        def samples(jt):
            return slice(jt * P, (jt + 1) * P)

        def term_tile(name, tag=None):
            return keep.tile([P, PACK, P], F32, name=name, tag=tag or name, align_bytes=64)

        def scaled(term, product, factor):
            nc.scalar.activation(term, product, ACT.Copy, scale=factor)
            return term

        def scaled_onto(term, product, factor, other):
            nc.vector.scalar_tensor_tensor(term, product, factor, other, ALU.mult, ALU.add)
            return term

        totals = {}

        def turn(term, jt, first, last):
            if first:
                totals[jt] = products.tile([P, PACK, P], F32, name="total%d" % jt, tag="bank%d" % jt)
            for t in range(PACK):
                nc.tensor.matmul(
                    totals[jt][:, t, :], term[:, t, :], ident[:],
                    start=(first and t == 0), stop=(last and t == PACK - 1), is_transpose=True,
                )

        near_es = gather("near_es", es, fine_t[:], U8, tag="w1_bf0")
        far_es = gather("far_es", es, ffar_t[:], U8)
        w2_q = quantize("w2", w2_bf)
        near_ew = gather("near_ew", ew, fine_t[:], U32, tag="w2_bf1")
        far_ew = [gather("far_ew%d" % h, ew, ffar_t[:, 16 * h : 16 * (h + 1)], U32) for h in range(2)]

        coarse = keep.tile([P, 2 * TILES, PACK, P], F32, name="coarse", tag="w2_raw1", align_bytes=64)
        near_y = coarse[:, :TILES]
        far_y, near_p, last = {}, {}, {}

        def near_coarse(jt):
            product = project(near_x[0][:, samples(jt)], near_x[1][:, samples(jt)], w1_q, jt)
            scaled(near_y[:, jt], product, near_w[:, jt : jt + 1])

        def far_coarse(jt):
            product = project(far_x[0][:, samples(jt)], far_x[1][:, samples(jt)], w1_q, TILES + jt)
            far_y[jt] = scaled(coarse[:, TILES + jt], product, far_w[:, jt : jt + 1])

        def near_fine(jt, bank, chained, tag=None):
            product = project(near_ew[:, samples(jt)], near_es[:, samples(jt)], w2_q, TILES + bank)
            factor = near_w[:, TILES + jt : TILES + jt + 1]
            if chained:
                near_p[jt] = scaled_onto(term_tile("near_p%d" % jt, tag)[:], product, factor, far_y[jt])
            else:
                near_p[jt] = scaled(term_tile("near_p%d" % jt)[:], product, factor)

        def far_fine(jt, bank, chained=True):
            product = project(far_ew[jt // 2][:, samples(jt % 2)], far_es[:, samples(jt)], w2_q, TILES + bank)
            factor = far_w[:, TILES + jt : TILES + jt + 1]
            if chained:
                last[jt] = scaled_onto(term_tile("far_p%d" % jt)[:], product, factor, near_p[jt])
            else:
                last[jt] = scaled(term_tile("far_p%d" % jt)[:], product, factor)

        hidden = [keep.tile([P, len(group), P, PACK], BF16, name="hidden%d" % group[0], align_bytes=64) for group in GROUPS]

        def rectify(jt):
            turn(last[jt], jt, False, True)
            total = totals[jt][:].rearrange("p t j -> p j t")
            target = [tile[:, group.index(jt)] for group, tile in zip(GROUPS, hidden) if jt in group][0]
            if jt < SCALAR_RELUS:
                nc.scalar.activation(target, total, ACT.Relu)
            else:
                nc.vector.tensor_scalar_max(target, total, 0.0)

        near_coarse(0)
        near_coarse(1)
        near_coarse(2)
        near_coarse(3)
        far_coarse(0)
        far_coarse(1)
        far_coarse(2)
        far_coarse(3)
        turn(near_y[:, 0], 0, True, False)
        turn(near_y[:, 1], 1, True, False)
        turn(near_y[:, 2], 2, True, False)
        turn(near_y[:, 3], 3, True, False)
        turn(far_y[0], 0, False, False)
        near_fine(0, 0, False)
        near_fine(2, 1, True, "ew")
        turn(far_y[1], 1, False, False)
        near_fine(3, 2, True)
        near_fine(1, 3, False)
        far_fine(0, 1)
        far_fine(1, 0)
        far_fine(2, 2)
        rectify(0)
        far_fine(3, 3)
        w3_q = quantize("w3", [interleave("w3_bf", w3_raw, nc.scalar.copy, tag="near_p0")])
        rectify(1)
        rectify(2)
        rectify(3)
        for group, tile in zip(GROUPS, hidden):
            width = len(group) * P
            codes = keep.tile([P, width], U32, name="h_codes%d" % group[0], align_bytes=64)
            scales = keep.tile([P, width], U8, name="h_scales%d" % group[0], align_bytes=64)
            nc.vector.quantize_mx(out=codes[:].bitcast(FP8X4), scales=scales[:], in_=tile[:].rearrange("p g j t -> p (g j t)"))
            logits = products.tile([P, H], F32, name="logits", tag="bank%d" % (TILES + group[0]))
            nc.tensor.matmul_mx(
                out=logits[:, 0:width],
                lhsT=w3_q[0][:].bitcast(FP8X4),
                lhsT_scale=w3_q[1][:],
                rhs=codes[:].bitcast(FP8X4),
                rhs_scale=scales[:],
                start=True,
                stop=True,
            )
            result = keep.tile([P, width], F32, name="result%d" % group[0])
            nc.scalar.activation(result[:], logits[:, 0:width], ACT.Sigmoid)
            nc.sync.dma_start(out[:, group[0] * P : group[0] * P + width], result[:])
